import numpy as np
import ml_dtypes


def mxq(x, axis, fmt="e4m3"):
    dtype, down = {"e4m3": (ml_dtypes.float8_e4m3fn, 7), "e5m2": (ml_dtypes.float8_e5m2, 14)}[fmt]
    v = np.moveaxis(np.asarray(x, np.float32).astype(ml_dtypes.bfloat16).astype(np.float64), axis, -1)
    blocks = v.reshape(v.shape[:-1] + (-1, 32))
    amax = np.abs(blocks).max(-1, keepdims=True)
    byte = np.maximum(np.where(amax > 0, np.frexp(amax)[1] - 1 + 127, 0) - down, 1)
    scale = np.exp2(byte - 127.0)
    codes = (blocks / scale).astype(np.float32).astype(dtype).astype(np.float64)
    return np.moveaxis((codes * scale).reshape(v.shape), -1, axis)


WIDE = False


def mx_kscale(k):
    if not WIDE:
        return np.ones(k)
    levels = np.array([10, -10, 5, -5, 0])
    if k % 512:
        return np.exp2(np.random.permutation(np.resize(levels, k // 32))).repeat(32)
    a = np.empty((k // 512, 16))
    for p in range(k // 512):
        a[p, :8] = np.random.permutation(np.resize(levels, 8))
        for g in range(8):
            far = levels[np.abs(levels - a[p, g]) >= 10]
            a[p, g + 8] = far[np.random.randint(len(far))]
    return np.exp2(a.ravel()).repeat(32)


def f64(x):
    return np.asarray(x).astype(np.float64)


def striped(idx):
    return np.tile(idx.reshape(-1, 16).T, (8, 1)).astype(np.uint16)


def unstriped(offs):
    return offs[:16].T.reshape(-1).astype(np.int64)


def striped8(idx):
    return np.concatenate([x.reshape(-1, 16).T for x in idx]).astype(np.uint16)


def runs(offs, k):
    lists = np.stack([offs[16 * r : 16 * r + 16].T.reshape(-1) for r in range(8)]).astype(np.int64)
    return lists[np.arange(k) % 512 // 64]


def pack_weight(w):
    k, n = w.shape
    w = f64(np.asarray(w, np.float32).astype(ml_dtypes.bfloat16)).reshape(k // 32, 32, n)
    amax = np.abs(w).max(1)
    byte = np.clip(np.where(amax > 0, np.frexp(amax)[1] - 1 + 127 - 7, 1), 1, 254)
    scaled = (w * np.exp2(127.0 - byte)[:, None, :]).reshape(k, n).astype(np.float32)
    words = np.ascontiguousarray(scaled.reshape(k // 512, 128, 4, n).transpose(0, 1, 3, 2)).astype(ml_dtypes.float8_e4m3fn).view(np.uint8)
    return words, np.ascontiguousarray(byte.astype(np.uint8).reshape(k // 512, 16, n))


def unpack_weight(words, scales):
    g, p, n, _ = words.shape
    vals = np.ascontiguousarray(words).view(ml_dtypes.float8_e4m3fn).astype(np.float64) * np.repeat(np.exp2(scales.astype(np.float64) - 127.0), 8, axis=1)[..., None]
    return vals.transpose(0, 1, 3, 2).reshape(g * 512, n)


E2M1 = np.array([0.0, 0.5, 1.0, 1.5, 2.0, 3.0, 4.0, 6.0, -0.0, -0.5, -1.0, -1.5, -2.0, -3.0, -4.0, -6.0])


def pack_fp4(w):
    k, n = w.shape
    w = f64(np.asarray(w, np.float32).astype(ml_dtypes.bfloat16)).reshape(k // 32, 32, n)
    amax = np.abs(w).max(1)
    mant, ex = np.frexp(amax / 6.0)
    byte = np.clip(np.where(amax > 0, np.where(mant > 0.5, ex, ex - 1) + 127, 1), 1, 254)
    scaled = (w * np.exp2(127.0 - byte)[:, None, :]).reshape(k, n).astype(np.float32)
    c = np.ascontiguousarray(scaled.reshape(k // 512, 128, 4, n).transpose(0, 1, 3, 2)).astype(ml_dtypes.float4_e2m1fn).view(np.uint8) & 0xF
    words = (c[..., 0::2] | (c[..., 1::2] << 4)).reshape(k // 512, 128, 2 * n)
    return np.ascontiguousarray(words), np.ascontiguousarray(byte.astype(np.uint8).reshape(k // 512, 16, n))


def unpack_fp4(words, scales):
    g, _, n = scales.shape
    words = np.ascontiguousarray(words).reshape(g, 128, n, 2)
    nib = np.empty((g, 128, n, 4), np.uint8)
    nib[..., 0::2] = words & 0xF
    nib[..., 1::2] = words >> 4
    vals = E2M1[nib] * np.repeat(np.exp2(scales.astype(np.float64) - 127.0), 8, axis=1)[..., None]
    return vals.transpose(0, 1, 3, 2).reshape(g * 512, n)


K, T, S, N, G, H, W = 512, 1024, 512, 512, 2048, 512, 256


def setup_inputs():
    n = np.random.standard_normal
    s = mx_kscale(K)[:, None]
    u = mx_kscale(S)
    packed_xT = pack_weight(n((K, T)) * s)
    packed_dT = pack_weight(n((K, G)) / s)
    packed_w1 = pack_fp4(n((H, N)) / np.sqrt(2 * H) / u[:, None])
    packed_w2 = pack_fp4(n((K, N)) / np.sqrt(2 * K) / s)
    perm = np.stack([np.random.permutation(S) for _ in range(8)])
    perm2 = np.stack([np.random.permutation(S) for _ in range(8)])
    perm3 = np.stack([np.random.permutation(S) for _ in range(8)])
    return {
        "x_words": packed_xT[0],
        "x_scales": packed_xT[1],
        "d_words": packed_dT[0],
        "d_scales": packed_dT[1],
        "gn": (np.random.uniform(0.5, 1.5, (H, 1)) * u[:, None]).astype(np.float32),
        "w1_words": packed_w1[0],
        "w1_scales": packed_w1[1],
        "w2_words": packed_w2[0],
        "w2_scales": packed_w2[1],
        "offs": striped(np.random.permutation(T)[:S]),
        "k1": striped8(np.random.randint(0, G, (8, H))),
        "hz": striped8(np.random.randint(0, T, (8, S))),
        "k2": striped8(np.random.randint(0, G, (8, H))),
        "hy": striped8(np.random.randint(0, T, (8, S))),
        "k3": striped8(np.random.randint(0, G, (8, H))),
        "n1": striped8(perm[:, :W]),
        "n2": striped8(perm[:, W:]),
        "hx": striped8(np.random.randint(0, T, (8, S))),
        "n3": striped8(perm2[:, :W]),
        "n4": striped8(perm2[:, W:]),
        "n5": striped8(perm3[:, :W]),
        "n6": striped8(perm3[:, W:]),
    }


def reference(x_words, x_scales, d_words, d_scales, gn, w1_words, w1_scales, w2_words, w2_scales, offs, k1, hz, k2, hy, k3, n1, n2, hx, n3, n4, n5, n6):
    d_k1 = unpack_weight(d_words, d_scales)[np.arange(K)[:, None], runs(k1, K)]
    xq = unpack_weight(x_words, x_scales)[:, unstriped(offs)]
    d_k2 = unpack_weight(d_words, d_scales)[np.arange(K)[:, None], runs(k2, K)]
    x_hz = unpack_weight(x_words, x_scales)[np.arange(K)[:, None], runs(hz, K)]
    d_k3 = unpack_weight(d_words, d_scales)[np.arange(K)[:, None], runs(k3, K)]
    x_hy = unpack_weight(x_words, x_scales)[np.arange(K)[:, None], runs(hy, K)]
    h = 0.0625 * (d_k1.T @ xq + d_k2.T @ x_hz + d_k3.T @ x_hy)
    pa = h[np.arange(H)[:, None], runs(n1, H)]
    pb = h[np.arange(H)[:, None], runs(n2, H)]
    rb = pa - pb
    ra = 0.75 * (pa + pb)
    ua = np.zeros((H, S))
    ua[np.arange(H)[:, None], runs(n1, H)] = ra
    ub = ua.copy()
    ub[np.arange(H)[:, None], runs(n2, H)] = rb
    z = f64(gn) * ub
    x_hx = unpack_weight(x_words, x_scales)[np.arange(K)[:, None], runs(hx, K)]
    h2 = unpack_fp4(w1_words, w1_scales).T @ mxq(z, 0, "e4m3") + unpack_fp4(w2_words, w2_scales).T @ x_hx
    pa2 = h2[np.arange(N)[:, None], runs(n3, N)]
    pb2 = h2[np.arange(N)[:, None], runs(n4, N)]
    rb2 = np.minimum(pa2, pb2)
    ra2 = np.maximum(pa2, pb2)
    ua2 = np.zeros((N, S))
    ua2[np.arange(N)[:, None], runs(n5, N)] = ra2
    ub2 = ua2.copy()
    ub2[np.arange(N)[:, None], runs(n6, N)] = rb2
    return ub2 - h2

@@ -1,0 +1,266 @@
+from contextlib import ExitStack
+
+import concourse.mybir as mybir
+
+F32 = mybir.dt.float32
+BF16 = mybir.dt.bfloat16
+I32 = mybir.dt.int32
+U32 = mybir.dt.uint32
+U16 = mybir.dt.uint16
+U8 = mybir.dt.uint8
+FP8X4 = mybir.dt.float8_e4m3fn_x4
+FP4X4 = mybir.dt.float4_e2m1fn_x4
+ALU = mybir.AluOpType
+ACT = mybir.ActivationFunctionType
+
+P = 128
+PACK = 4
+T, G, S, W = 1024, 2048, 512, 256
+HALF = S // 2
+FLOPS = 5 * 2 * 512 * 512 * 512
+
+
+def dealt_pair(dst, src, run):
+    return (dst.rearrange("p (t c i) -> p c t i", t=PACK, i=run),
+            src.rearrange("p (c i t) -> p c t i", t=PACK, i=run))
+
+
+def tile_picked_mthhznhhaarcpor_none_p_kernel(
+    tc, x_words, x_scales, d_words, d_scales, gn, w1_words, w1_scales, w2_words, w2_scales,
+    offs, k1, hz, k2, hy, k3, n1, n2, hx, n3, n4, n5, n6, out,
+):
+    nc = tc.nc
+    with ExitStack() as ctx:
+        lists = ctx.enter_context(tc.tile_pool(name="lists", bufs=1))
+        keep = ctx.enter_context(tc.tile_pool(name="keep", bufs=1))
+        psum = ctx.enter_context(tc.psum_pool(name="psum", bufs=1))
+
+        def sbuf(name, cols, dtype, tag=None):
+            return keep.tile([P, cols], dtype, name=name, tag=tag or name, align_bytes=64)
+
+        def load_list(name, src):
+            tile = lists.tile(list(src.shape), U16, name=name)
+            nc.sync.dma_start(tile[:], src)
+            return tile
+
+        def zeroed(name, cols, tag=None):
+            tile = sbuf(name, cols, U8, tag)
+            nc.vector.memset(tile[:].bitcast(I32), 0)
+            return tile
+
+        def move_rows(dst, dst_first, src, src_first=0):
+            for s in range(4):
+                nc.sync.dma_start(dst[dst_first + s : P : 32, :].bitcast(I32),
+                                  src[src_first + 8 * s : P : 32, :].bitcast(I32))
+
+        ds_table = zeroed("ds_table", G)
+        nc.sync.dma_start(ds_table[0:P:8, :].bitcast(I32), d_scales[0].bitcast(I32))
+        d_lists = [load_list("k1", k1), load_list("k2", k2), load_list("k3", k3)]
+        xs_table = zeroed("xs_table", T)
+        nc.sync.dma_start(xs_table[0:P:8, :].bitcast(I32), x_scales[0].bitcast(I32))
+        x_lists = [load_list("offs", offs), load_list("hz", hz), load_list("hy", hy)]
+        dw_table = sbuf("dw_table", G, U32)
+        nc.sync.dma_start(dw_table[:].bitcast(I32), d_words[0].rearrange("p n t -> p (n t)").bitcast(I32))
+        xw_table = sbuf("xw_table", T, U32)
+        nc.sync.dma_start(xw_table[:].bitcast(I32), x_words[0].rearrange("p n t -> p (n t)").bitcast(I32))
+        ds_placed = zeroed("ds_placed", S, tag="slot3")
+        xs_placed = zeroed("xs_placed", 3 * S)
+        hxs_placed = zeroed("hxs_placed", S)
+        ws_raw = zeroed("ws_raw", S)
+        ws_placed = [zeroed("w1s_placed", S), zeroed("w2s_placed", S)]
+
+        for a in range(3):
+            ds_picked = sbuf(f"ds_picked{a}", S, U8, tag=f"slot{a}")
+            nc.vector.tensor_copy(ds_picked[:], ds_table[:].indirect(d_lists[a][:]))
+            move_rows(ds_placed, 4 * a, ds_picked)
+        xs_picked = sbuf("xs_picked", 3 * S, U8)
+        for a in range(3):
+            nc.vector.tensor_copy(xs_picked[:, a * S : (a + 1) * S], xs_table[:].indirect(x_lists[a][:]))
+        move_rows(xs_placed, 0, xs_picked)
+
+        gain_raw = sbuf("gain_raw", PACK, F32)
+        nc.sync.dma_start(gain_raw[:], gn.rearrange("(p t) o -> p (t o)", t=PACK))
+        l_n1, l_n2, l_hx = load_list("n1", n1), load_list("n2", n2), load_list("hx", hx)
+        w_dealt = []
+        for w, (words, scales) in enumerate(((w1_words, w1_scales), (w2_words, w2_scales))):
+            raw = sbuf(f"w_raw{w}", 2 * S, U8)
+            nc.sync.dma_start(raw[:].bitcast(I32), words[0].bitcast(I32))
+            nc.sync.dma_start(ws_raw[w:P:8, :].bitcast(I32), scales[0].bitcast(I32))
+            dealt = sbuf(f"w_dealt{w}", 2 * S, U8)
+            nc.scalar.copy(*dealt_pair(dealt[:].bitcast(U16), raw[:].bitcast(U16), 8))
+            w_dealt.append(dealt)
+        l_n3, l_n4, l_n5, l_n6 = load_list("n3", n3), load_list("n4", n4), load_list("n5", n5), load_list("n6", n6)
+        gain = sbuf("gain", PACK, F32)
+        nc.scalar.activation(gain[:], gain_raw[:], ACT.Copy, scale=0.0625 * 0.75)
+
+        ds_dealt = sbuf("ds_dealt", S, U8)
+        h_banks = [psum.tile([P, S], F32, name=f"h_bank{t}", tag=f"bank{t}") for t in range(PACK)]
+        dw_dealt, xw_picked = [], []
+
+        def first_pass(a, t):
+            cols = slice(t * P, (t + 1) * P)
+            nc.tensor.matmul_mx(
+                out=h_banks[t][:], lhsT=dw_dealt[a][:, cols].bitcast(FP8X4), lhsT_scale=ds_dealt[4 * a : P, cols],
+                rhs=xw_picked[a][:].bitcast(FP8X4), rhs_scale=xs_placed[:, a * S : (a + 1) * S],
+                start=(a == 0), stop=(a == 2))
+
+        nc.vector.tensor_copy(*dealt_pair(ds_dealt[:], ds_placed[:], 16))
+        for a, (dw_slot, xw_slot) in enumerate(((0, 1), (2, 3), (0, 2))):
+            picked = sbuf(f"dw_picked{a}", S, U32, tag=f"slot{dw_slot}")
+            nc.vector.tensor_copy(picked[:], dw_table[:].indirect(d_lists[a][:]))
+            xw_picked.append(sbuf(f"xw_picked{a}", S, U32, tag=f"slot{xw_slot}"))
+            nc.vector.tensor_copy(xw_picked[a][:], xw_table[:].indirect(x_lists[a][:]))
+            dw_dealt.append(sbuf(f"dw_dealt{a}", S, U32))
+            nc.vector.tensor_copy(*dealt_pair(dw_dealt[a][:].bitcast(I32), picked[:].bitcast(I32), 4))
+            for t in (1, 3, 0, 2):
+                first_pass(a, t)
+
+        hxw = sbuf("hxw", S, U32, tag="slot3")
+        nc.vector.tensor_copy(hxw[:], xw_table[:].indirect(l_hx[:]))
+        hxs_picked = sbuf("hxs_picked", S, U8, tag="dw_dealt1")
+        nc.vector.tensor_copy(hxs_picked[:], xs_table[:].indirect(l_hx[:]))
+        move_rows(hxs_placed, 0, hxs_picked)
+        ws_dealt = sbuf("ws_dealt", S, U8, tag="slot2")
+        nc.vector.tensor_copy(*dealt_pair(ws_dealt[:], ws_raw[:], 16))
+        for w in range(2):
+            move_rows(ws_placed[w], 0, ws_dealt, w)
+
+        h = [sbuf(f"h{t}", S, F32) for t in range(PACK)]
+        terms = [sbuf(f"terms{t}", 4 * W, F32) for t in range(PACK)]
+        z = [sbuf(f"z{t}", S * (2 - t % 2), F32) for t in range(PACK)]
+
+        def empty_h(t):
+            nc.scalar.activation(h[t][:], h_banks[t][:], ACT.Copy, scale=gain[:, t : t + 1])
+
+        def fetch_pairs(t):
+            nc.scalar.activation(terms[t][:, 0:W], h[t][:].indirect(l_n1[:]), ACT.Copy)
+            nc.scalar.activation(terms[t][:, W : 2 * W], h[t][:].indirect(l_n2[:]), ACT.Copy)
+
+        def rescale(t):
+            nc.scalar.activation(terms[t][:, 2 * W : 3 * W], terms[t][:, 0:W], ACT.Copy, scale=4.0 / 3.0)
+            nc.scalar.activation(terms[t][:, 3 * W :], terms[t][:, W : 2 * W], ACT.Copy, scale=-4.0 / 3.0)
+
+        def put_sum(t):
+            nc.vector.tensor_tensor(z[t][:].indirect(l_n1[:]), terms[t][:, 0:W], terms[t][:, W : 2 * W], ALU.add)
+
+        def put_diff(t):
+            nc.vector.tensor_tensor(z[t][:].indirect(l_n2[:]), terms[t][:, 2 * W : 3 * W], terms[t][:, 3 * W :], ALU.add)
+
+        z_bf = sbuf("z_bf", PACK * S, BF16)
+
+        def round_pair(copy, t, c0, c1):
+            dst = z_bf[:].rearrange("p (j u e) -> p j u e", u=2, e=2)[:, c0:c1, t // 2, :]
+            src = z[t][:].rearrange("p (e j) -> p j e", e=2)[:, c0:c1, :]
+            copy(dst, src)
+
+        empty_h(1)
+        fetch_pairs(1)
+        put_sum(1)
+        empty_h(3)
+        rescale(1)
+        put_diff(1)
+        fetch_pairs(3)
+        put_sum(3)
+        empty_h(0)
+        nc.scalar.copy(z[0][:, S:], z[1][:])
+        fetch_pairs(0)
+        put_sum(0)
+        rescale(3)
+        put_diff(3)
+        rescale(0)
+        put_diff(0)
+        empty_h(2)
+        fetch_pairs(2)
+        nc.scalar.copy(z[2][:, S:], z[3][:])
+        put_sum(2)
+        rescale(2)
+
+        chunks = [[(0, HALF), (HALF, S)]] + [[(0, S)]] * 3
+        h2_banks = []
+        bank_no = 4
+        for t in range(PACK):
+            row = []
+            for c0, c1 in chunks[t]:
+                bank = psum.tile([P, c1 - c0], F32, name=f"h2_bank{t}_{c0}", tag=f"bank{bank_no % 8}")
+                bank_no += 1
+                nc.tensor.matmul_mx(
+                    out=bank[:], lhsT=w_dealt[1][:, 2 * t * P : 2 * (t + 1) * P].bitcast(FP4X4),
+                    lhsT_scale=ws_placed[1][:, t * P : (t + 1) * P],
+                    rhs=hxw[:, c0:c1].bitcast(FP8X4), rhs_scale=hxs_placed[:, c0:c1], start=True, stop=False)
+                row.append(bank)
+            h2_banks.append(row)
+
+        round_pair(nc.scalar.copy, 0, 0, S)
+        put_diff(2)
+        round_pair(nc.vector.tensor_copy, 2, 0, HALF)
+        round_pair(nc.scalar.copy, 2, 384, S)
+        round_pair(nc.vector.tensor_copy, 2, HALF, 384)
+        zw = sbuf("zw", S, U32)
+        zs = sbuf("zs", S, U8)
+        for c0, c1 in chunks[0]:
+            nc.vector.quantize_mx(out=zw[:, c0:c1].bitcast(FP8X4), scales=zs[:, c0:c1], in_=z_bf[:, PACK * c0 : PACK * c1])
+        for t in range(PACK):
+            for (c0, c1), bank in zip(chunks[t], h2_banks[t]):
+                nc.tensor.matmul_mx(
+                    out=bank[:], lhsT=w_dealt[0][:, 2 * t * P : 2 * (t + 1) * P].bitcast(FP4X4),
+                    lhsT_scale=ws_placed[0][:, t * P : (t + 1) * P],
+                    rhs=zw[:, c0:c1].bitcast(FP8X4), rhs_scale=zs[:, c0:c1], start=False, stop=True)
+
+        h2 = [sbuf(f"h2_{t}", S, F32) for t in range(PACK)]
+        pair = [sbuf(f"pair{t}", 2 * W, F32) for t in range(PACK)]
+        rise = [sbuf(f"rise{t}", 3 * W, F32) for t in range(PACK)]
+        ub2 = [sbuf(f"ub2_{t}", S, F32) for t in range(PACK)]
+        out_rows = out.rearrange("(p t) j -> p t j", t=PACK)
+
+        def empty(t):
+            nc.scalar.copy(h2[t][:], h2_banks[t][0][:])
+
+        def fetch(t):
+            nc.scalar.activation(pair[t][:, 0:W], h2[t][:].indirect(l_n3[:]), ACT.Copy)
+            nc.scalar.activation(pair[t][:, W:], h2[t][:].indirect(l_n4[:]), ACT.Copy)
+
+        def diff(t):
+            nc.vector.tensor_tensor(rise[t][:, 0:W], pair[t][:, W:], pair[t][:, 0:W], ALU.subtract)
+
+        def clip(t):
+            nc.scalar.activation(rise[t][:, W : 2 * W], rise[t][:, 0:W], ACT.Relu)
+            nc.scalar.activation(rise[t][:, 2 * W :], rise[t][:, W : 2 * W], ACT.Copy, scale=-1.0)
+
+        def put_max(t):
+            nc.vector.tensor_tensor(ub2[t][:].indirect(l_n5[:]), pair[t][:, 0:W], rise[t][:, W : 2 * W], ALU.add)
+
+        def put_min(t):
+            nc.vector.tensor_tensor(ub2[t][:].indirect(l_n6[:]), pair[t][:, W:], rise[t][:, 2 * W :], ALU.add)
+
+        def finish(t, pieces):
+            res = sbuf(f"res{t}", S, F32)
+            for c0, c1 in pieces:
+                nc.vector.tensor_tensor(res[:, c0:c1], ub2[t][:, c0:c1], h2[t][:, c0:c1], ALU.subtract)
+                nc.sync.dma_start(out_rows[:, t, c0:c1], res[:, c0:c1])
+
+        nc.scalar.copy(h2[0][:, :HALF], h2_banks[0][0][:])
+        nc.vector.tensor_copy(h2[0][:, HALF:], h2_banks[0][1][:])
+        nc.scalar.activation(pair[0][:, 0:W], h2[0][:].indirect(l_n3[:]), ACT.Copy)
+        nc.vector.tensor_copy(pair[0][:, W:], h2[0][:].indirect(l_n4[:]))
+        nc.vector.tensor_tensor(rise[0][:, 0:W], pair[0][:, 0:W], pair[0][:, W:], ALU.max)
+        nc.vector.tensor_tensor(rise[0][:, W : 2 * W], pair[0][:, 0:W], pair[0][:, W:], ALU.min)
+        empty(1)
+        fetch(1)
+        nc.vector.tensor_copy(ub2[0][:].indirect(l_n5[:]), rise[0][:, 0:W])
+        diff(1)
+        empty(2)
+        clip(1)
+        fetch(2)
+        nc.vector.tensor_copy(ub2[0][:].indirect(l_n6[:]), rise[0][:, W : 2 * W])
+        for t in range(1, PACK):
+            put_max(t)
+            finish(t - 1, [(0, S)])
+            if t + 1 < PACK:
+                diff(t + 1)
+                if t + 2 < PACK:
+                    empty(t + 2)
+                clip(t + 1)
+                if t + 2 < PACK:
+                    fetch(t + 2)
+            put_min(t)
+        finish(PACK - 1, [(0, HALF), (HALF, S)])

@@ -53,24 +53,26 @@ def tile_picked_mthhznhhaarcpor_none_p_kernel(
                 nc.sync.dma_start(dst[dst_first + s : P : 32, :].bitcast(I32),
                                   src[src_first + 8 * s : P : 32, :].bitcast(I32))
 
-        ds_table = zeroed("ds_table", G)
+        ds_table = sbuf("ds_table", G, U8)
+        nc.gpsimd.memset(ds_table[:, : G // 2].bitcast(I32), 0)
+        nc.vector.memset(ds_table[:, G // 2 :].bitcast(I32), 0)
         nc.sync.dma_start(ds_table[0:P:8, :].bitcast(I32), d_scales[0].bitcast(I32))
         d_lists = [load_list("k1", k1), load_list("k2", k2), load_list("k3", k3)]
         xs_table = zeroed("xs_table", T)
         nc.sync.dma_start(xs_table[0:P:8, :].bitcast(I32), x_scales[0].bitcast(I32))
         x_lists = [load_list("offs", offs), load_list("hz", hz), load_list("hy", hy)]
-        dw_table = sbuf("dw_table", G, U32)
-        nc.sync.dma_start(dw_table[:].bitcast(I32), d_words[0].rearrange("p n t -> p (n t)").bitcast(I32))
         xw_table = sbuf("xw_table", T, U32)
         nc.sync.dma_start(xw_table[:].bitcast(I32), x_words[0].rearrange("p n t -> p (n t)").bitcast(I32))
-        ds_placed = zeroed("ds_placed", S, tag="slot3")
+        dw_table = sbuf("dw_table", G, U32)
+        nc.sync.dma_start(dw_table[:].bitcast(I32), d_words[0].rearrange("p n t -> p (n t)").bitcast(I32))
+        ds_placed = zeroed("ds_placed", S, tag="slot_b")
         xs_placed = zeroed("xs_placed", 3 * S)
         hxs_placed = zeroed("hxs_placed", S)
         ws_raw = zeroed("ws_raw", S)
         ws_placed = [zeroed("w1s_placed", S), zeroed("w2s_placed", S)]
 
         for a in range(3):
-            ds_picked = sbuf(f"ds_picked{a}", S, U8, tag=f"slot{a}")
+            ds_picked = sbuf(f"ds_picked{a}", S, U8, tag="slot_a" if a == 2 else None)
             nc.vector.tensor_copy(ds_picked[:], ds_table[:].indirect(d_lists[a][:]))
             move_rows(ds_placed, 4 * a, ds_picked)
         xs_picked = sbuf("xs_picked", 3 * S, U8)
@@ -104,26 +106,34 @@ def tile_picked_mthhznhhaarcpor_none_p_kernel(
                 rhs=xw_picked[a][:].bitcast(FP8X4), rhs_scale=xs_placed[:, a * S : (a + 1) * S],
                 start=(a == 0), stop=(a == 2))
 
-        nc.vector.tensor_copy(*dealt_pair(ds_dealt[:], ds_placed[:], 16))
-        for a, (dw_slot, xw_slot) in enumerate(((0, 1), (2, 3), (0, 2))):
-            picked = sbuf(f"dw_picked{a}", S, U32, tag=f"slot{dw_slot}")
-            nc.vector.tensor_copy(picked[:], dw_table[:].indirect(d_lists[a][:]))
-            xw_picked.append(sbuf(f"xw_picked{a}", S, U32, tag=f"slot{xw_slot}"))
+        def pick_x(a, tag=None):
+            xw_picked.append(sbuf(f"xw_picked{a}", S, U32, tag))
             nc.vector.tensor_copy(xw_picked[a][:], xw_table[:].indirect(x_lists[a][:]))
+
+        def pick_d(a, tag):
+            picked = sbuf(f"dw_picked{a}", S, U32, tag)
+            nc.vector.tensor_copy(picked[:], dw_table[:].indirect(d_lists[a][:]))
+            return picked
+
+        def deal_d(a, picked):
             dw_dealt.append(sbuf(f"dw_dealt{a}", S, U32))
             nc.vector.tensor_copy(*dealt_pair(dw_dealt[a][:].bitcast(I32), picked[:].bitcast(I32), 4))
-            for t in (1, 3, 0, 2):
+
+        pick_x(0)
+        pick_x(1)
+        nc.vector.tensor_copy(*dealt_pair(ds_dealt[:], ds_placed[:], 16))
+        picked = [pick_d(0, "slot_a"), pick_d(1, "slot_b")]
+        deal_d(0, picked[0])
+        deal_d(1, picked[1])
+        picked.append(pick_d(2, "slot_a"))
+        pick_x(2, "slot_b")
+        deal_d(2, picked[2])
+        for t in (1, 3, 0, 2):
+            for a in range(3):
                 first_pass(a, t)
 
-        hxw = sbuf("hxw", S, U32, tag="slot3")
+        hxw = sbuf("hxw", S, U32, tag="slot_a")
         nc.vector.tensor_copy(hxw[:], xw_table[:].indirect(l_hx[:]))
-        hxs_picked = sbuf("hxs_picked", S, U8, tag="dw_dealt1")
-        nc.vector.tensor_copy(hxs_picked[:], xs_table[:].indirect(l_hx[:]))
-        move_rows(hxs_placed, 0, hxs_picked)
-        ws_dealt = sbuf("ws_dealt", S, U8, tag="slot2")
-        nc.vector.tensor_copy(*dealt_pair(ws_dealt[:], ws_raw[:], 16))
-        for w in range(2):
-            move_rows(ws_placed[w], 0, ws_dealt, w)
 
         h = [sbuf(f"h{t}", S, F32) for t in range(PACK)]
         terms = [sbuf(f"terms{t}", 4 * W, F32) for t in range(PACK)]
@@ -132,8 +142,11 @@ def tile_picked_mthhznhhaarcpor_none_p_kernel(
         def empty_h(t):
             nc.scalar.activation(h[t][:], h_banks[t][:], ACT.Copy, scale=gain[:, t : t + 1])
 
-        def fetch_pairs(t):
+        def fetch_n1(t):
             nc.scalar.activation(terms[t][:, 0:W], h[t][:].indirect(l_n1[:]), ACT.Copy)
+
+        def fetch_pairs(t):
+            fetch_n1(t)
             nc.scalar.activation(terms[t][:, W : 2 * W], h[t][:].indirect(l_n2[:]), ACT.Copy)
 
         def rescale(t):
@@ -154,24 +167,32 @@ def tile_picked_mthhznhhaarcpor_none_p_kernel(
             copy(dst, src)
 
         empty_h(1)
-        fetch_pairs(1)
-        put_sum(1)
+        fetch_n1(1)
+        nc.vector.tensor_copy(terms[1][:, W : 2 * W], h[1][:].indirect(l_n2[:]))
         empty_h(3)
+        put_sum(1)
+        hxs_picked = sbuf("hxs_picked", S, U8, tag="h1")
+        nc.vector.tensor_copy(hxs_picked[:], xs_table[:].indirect(l_hx[:]))
+        move_rows(hxs_placed, 0, hxs_picked)
         rescale(1)
         put_diff(1)
+        nc.sync.dma_start(z[0][:, S:], z[1][:])
         fetch_pairs(3)
         put_sum(3)
+        ws_dealt = sbuf("ws_dealt", S, U8, tag="h3")
+        nc.vector.tensor_copy(*dealt_pair(ws_dealt[:], ws_raw[:], 16))
+        for w in range(2):
+            move_rows(ws_placed[w], 0, ws_dealt, w)
         empty_h(0)
-        nc.scalar.copy(z[0][:, S:], z[1][:])
-        fetch_pairs(0)
-        put_sum(0)
         rescale(3)
         put_diff(3)
+        nc.sync.dma_start(z[2][:, S:], z[3][:])
+        fetch_pairs(0)
+        put_sum(0)
+        empty_h(2)
         rescale(0)
         put_diff(0)
-        empty_h(2)
         fetch_pairs(2)
-        nc.scalar.copy(z[2][:, S:], z[3][:])
         put_sum(2)
         rescale(2)
 
@@ -208,7 +229,7 @@ def tile_picked_mthhznhhaarcpor_none_p_kernel(
 
         h2 = [sbuf(f"h2_{t}", S, F32) for t in range(PACK)]
         pair = [sbuf(f"pair{t}", 2 * W, F32) for t in range(PACK)]
-        rise = [sbuf(f"rise{t}", 3 * W, F32) for t in range(PACK)]
+        rise = [sbuf(f"rise{t}", 2 * W, F32) for t in range(PACK)]
         ub2 = [sbuf(f"ub2_{t}", S, F32) for t in range(PACK)]
         out_rows = out.rearrange("(p t) j -> p t j", t=PACK)
 
@@ -219,48 +240,31 @@ def tile_picked_mthhznhhaarcpor_none_p_kernel(
             nc.scalar.activation(pair[t][:, 0:W], h2[t][:].indirect(l_n3[:]), ACT.Copy)
             nc.scalar.activation(pair[t][:, W:], h2[t][:].indirect(l_n4[:]), ACT.Copy)
 
-        def diff(t):
-            nc.vector.tensor_tensor(rise[t][:, 0:W], pair[t][:, W:], pair[t][:, 0:W], ALU.subtract)
+        def larger(t):
+            nc.vector.tensor_tensor(rise[t][:, 0:W], pair[t][:, 0:W], pair[t][:, W:], ALU.max)
 
-        def clip(t):
-            nc.scalar.activation(rise[t][:, W : 2 * W], rise[t][:, 0:W], ACT.Relu)
-            nc.scalar.activation(rise[t][:, 2 * W :], rise[t][:, W : 2 * W], ACT.Copy, scale=-1.0)
+        def smaller(t):
+            nc.vector.tensor_tensor(rise[t][:, W:], pair[t][:, 0:W], pair[t][:, W:], ALU.min)
 
-        def put_max(t):
-            nc.vector.tensor_tensor(ub2[t][:].indirect(l_n5[:]), pair[t][:, 0:W], rise[t][:, W : 2 * W], ALU.add)
-
-        def put_min(t):
-            nc.vector.tensor_tensor(ub2[t][:].indirect(l_n6[:]), pair[t][:, W:], rise[t][:, 2 * W :], ALU.add)
-
-        def finish(t, pieces):
+        def finish(engine, t, pieces):
             res = sbuf(f"res{t}", S, F32)
             for c0, c1 in pieces:
-                nc.vector.tensor_tensor(res[:, c0:c1], ub2[t][:, c0:c1], h2[t][:, c0:c1], ALU.subtract)
+                engine.tensor_tensor(res[:, c0:c1], ub2[t][:, c0:c1], h2[t][:, c0:c1], ALU.subtract)
                 nc.sync.dma_start(out_rows[:, t, c0:c1], res[:, c0:c1])
 
         nc.scalar.copy(h2[0][:, :HALF], h2_banks[0][0][:])
         nc.vector.tensor_copy(h2[0][:, HALF:], h2_banks[0][1][:])
         nc.scalar.activation(pair[0][:, 0:W], h2[0][:].indirect(l_n3[:]), ACT.Copy)
         nc.vector.tensor_copy(pair[0][:, W:], h2[0][:].indirect(l_n4[:]))
-        nc.vector.tensor_tensor(rise[0][:, 0:W], pair[0][:, 0:W], pair[0][:, W:], ALU.max)
-        nc.vector.tensor_tensor(rise[0][:, W : 2 * W], pair[0][:, 0:W], pair[0][:, W:], ALU.min)
-        empty(1)
-        fetch(1)
-        nc.vector.tensor_copy(ub2[0][:].indirect(l_n5[:]), rise[0][:, 0:W])
-        diff(1)
-        empty(2)
-        clip(1)
-        fetch(2)
-        nc.vector.tensor_copy(ub2[0][:].indirect(l_n6[:]), rise[0][:, W : 2 * W])
-        for t in range(1, PACK):
-            put_max(t)
-            finish(t - 1, [(0, S)])
+        larger(0)
+        for t in range(PACK):
+            nc.vector.tensor_copy(ub2[t][:].indirect(l_n5[:]), rise[t][:, 0:W])
+            smaller(t)
             if t + 1 < PACK:
-                diff(t + 1)
-                if t + 2 < PACK:
-                    empty(t + 2)
-                clip(t + 1)
-                if t + 2 < PACK:
-                    fetch(t + 2)
-            put_min(t)
-        finish(PACK - 1, [(0, HALF), (HALF, S)])
+                empty(t + 1)
+                fetch(t + 1)
+                larger(t + 1)
+            nc.vector.tensor_copy(ub2[t][:].indirect(l_n6[:]), rise[t][:, W:])
+            if t + 1 < PACK:
+                finish(nc.gpsimd, t, [(0, S)])
+        finish(nc.vector, PACK - 1, [(0, HALF), (HALF, S)])

@@ -227,9 +227,8 @@ def tile_picked_mthhznhhaarcpor_none_p_kernel(
                     lhsT_scale=ws_placed[0][:, t * P : (t + 1) * P],
                     rhs=zw[:, c0:c1].bitcast(FP8X4), rhs_scale=zs[:, c0:c1], start=False, stop=True)
 
-        h2 = [sbuf(f"h2_{t}", S, F32) for t in range(PACK)]
+        h2 = [sbuf(f"h2_{t}", S, F32, "zw" if t == 1 else None) for t in range(PACK)]
         pair = [sbuf(f"pair{t}", 2 * W, F32) for t in range(PACK)]
-        rise = [sbuf(f"rise{t}", 2 * W, F32) for t in range(PACK)]
         ub2 = [sbuf(f"ub2_{t}", S, F32) for t in range(PACK)]
         out_rows = out.rearrange("(p t) j -> p t j", t=PACK)
 
@@ -240,31 +239,65 @@ def tile_picked_mthhznhhaarcpor_none_p_kernel(
             nc.scalar.activation(pair[t][:, 0:W], h2[t][:].indirect(l_n3[:]), ACT.Copy)
             nc.scalar.activation(pair[t][:, W:], h2[t][:].indirect(l_n4[:]), ACT.Copy)
 
-        def larger(t):
-            nc.vector.tensor_tensor(rise[t][:, 0:W], pair[t][:, 0:W], pair[t][:, W:], ALU.max)
+        gap, rise, larger, smaller = {}, {}, {}, {}
 
-        def smaller(t):
-            nc.vector.tensor_tensor(rise[t][:, W:], pair[t][:, 0:W], pair[t][:, W:], ALU.min)
+        def subtract_pair(engine, t):
+            gap[t] = sbuf(f"gap{t}", W, F32)
+            engine.tensor_tensor(gap[t][:], pair[t][:, W:], pair[t][:, 0:W], ALU.subtract)
 
-        def finish(engine, t, pieces):
-            res = sbuf(f"res{t}", S, F32)
-            for c0, c1 in pieces:
-                engine.tensor_tensor(res[:, c0:c1], ub2[t][:, c0:c1], h2[t][:, c0:c1], ALU.subtract)
-                nc.sync.dma_start(out_rows[:, t, c0:c1], res[:, c0:c1])
+        def rank_larger(t):
+            rise[t] = sbuf(f"rise{t}", W, F32)
+            larger[t] = sbuf(f"larger{t}", W, F32)
+            nc.scalar.activation(rise[t][:], gap[t][:], ACT.Relu)
+            nc.gpsimd.tensor_tensor(larger[t][:], pair[t][:, 0:W], rise[t][:], ALU.add)
+
+        def rank_smaller(t, tag=None):
+            smaller[t] = sbuf(f"smaller{t}", W, F32, tag)
+            nc.gpsimd.tensor_tensor(smaller[t][:], pair[t][:, W:], rise[t][:], ALU.subtract)
+
+        def put_larger(t):
+            nc.vector.tensor_copy(ub2[t][:].indirect(l_n5[:]), larger[t][:])
+
+        def put_smaller(t):
+            nc.vector.tensor_copy(ub2[t][:].indirect(l_n6[:]), smaller[t][:])
+
+        def finish(engine, t, res, c0, c1):
+            engine.tensor_tensor(res[:, c0:c1], ub2[t][:, c0:c1], h2[t][:, c0:c1], ALU.subtract)
+            nc.sync.dma_start(out_rows[:, t, c0:c1], res[:, c0:c1])
 
         nc.scalar.copy(h2[0][:, :HALF], h2_banks[0][0][:])
         nc.vector.tensor_copy(h2[0][:, HALF:], h2_banks[0][1][:])
         nc.scalar.activation(pair[0][:, 0:W], h2[0][:].indirect(l_n3[:]), ACT.Copy)
         nc.vector.tensor_copy(pair[0][:, W:], h2[0][:].indirect(l_n4[:]))
-        larger(0)
-        for t in range(PACK):
-            nc.vector.tensor_copy(ub2[t][:].indirect(l_n5[:]), rise[t][:, 0:W])
-            smaller(t)
-            if t + 1 < PACK:
-                empty(t + 1)
-                fetch(t + 1)
-                larger(t + 1)
-            nc.vector.tensor_copy(ub2[t][:].indirect(l_n6[:]), rise[t][:, W:])
-            if t + 1 < PACK:
-                finish(nc.gpsimd, t, [(0, S)])
-        finish(nc.vector, PACK - 1, [(0, HALF), (HALF, S)])
+        larger[0] = sbuf("larger0", W, F32)
+        smaller[0] = sbuf("smaller0", W, F32)
+        nc.vector.tensor_tensor(larger[0][:], pair[0][:, 0:W], pair[0][:, W:], ALU.max)
+        nc.vector.tensor_tensor(smaller[0][:], pair[0][:, 0:W], pair[0][:, W:], ALU.min)
+        put_larger(0)
+        put_smaller(0)
+        empty(1)
+        fetch(1)
+        empty(2)
+        subtract_pair(nc.gpsimd, 1)
+        rank_larger(1)
+        put_larger(1)
+        rank_smaller(1)
+        put_smaller(1)
+        fetch(2)
+        empty(3)
+        subtract_pair(nc.gpsimd, 2)
+        rank_larger(2)
+        put_larger(2)
+        fetch(3)
+        subtract_pair(nc.gpsimd, 3)
+        rank_larger(3)
+        put_larger(3)
+        rank_smaller(2, "gap3")
+        put_smaller(2)
+        rank_smaller(3)
+        put_smaller(3)
+        for t, tag in enumerate(("rise3", "pair3", None)):
+            finish(nc.gpsimd, t, sbuf(f"res{t}", S, F32, tag), 0, S)
+        last = sbuf("res3", S, F32)
+        finish(nc.vector, PACK - 1, last, 0, HALF)
+        finish(nc.vector, PACK - 1, last, HALF, S)

@@ -227,12 +227,13 @@ def tile_picked_mthhznhhaarcpor_none_p_kernel(
                     lhsT_scale=ws_placed[0][:, t * P : (t + 1) * P],
                     rhs=zw[:, c0:c1].bitcast(FP8X4), rhs_scale=zs[:, c0:c1], start=False, stop=True)
 
-        h2 = [sbuf(f"h2_{t}", S, F32, "zw" if t == 1 else None) for t in range(PACK)]
+        h2 = [sbuf(f"h2_{t}", S, F32) for t in range(2)]
         pair = [sbuf(f"pair{t}", 2 * W, F32) for t in range(PACK)]
         ub2 = [sbuf(f"ub2_{t}", S, F32) for t in range(PACK)]
         out_rows = out.rearrange("(p t) j -> p t j", t=PACK)
 
-        def empty(t):
+        def empty(t, tag):
+            h2.append(sbuf(f"h2_{t}", S, F32, tag))
             nc.scalar.copy(h2[t][:], h2_banks[t][0][:])
 
         def fetch(t):
@@ -241,9 +242,9 @@ def tile_picked_mthhznhhaarcpor_none_p_kernel(
 
         gap, rise, larger, smaller = {}, {}, {}, {}
 
-        def subtract_pair(engine, t):
+        def subtract_pair(t):
             gap[t] = sbuf(f"gap{t}", W, F32)
-            engine.tensor_tensor(gap[t][:], pair[t][:, W:], pair[t][:, 0:W], ALU.subtract)
+            nc.gpsimd.tensor_tensor(gap[t][:], pair[t][:, W:], pair[t][:, 0:W], ALU.subtract)
 
         def rank_larger(t):
             rise[t] = sbuf(f"rise{t}", W, F32)
@@ -267,6 +268,7 @@ def tile_picked_mthhznhhaarcpor_none_p_kernel(
 
         nc.scalar.copy(h2[0][:, :HALF], h2_banks[0][0][:])
         nc.vector.tensor_copy(h2[0][:, HALF:], h2_banks[0][1][:])
+        nc.vector.tensor_copy(h2[1][:], h2_banks[1][0][:])
         nc.scalar.activation(pair[0][:, 0:W], h2[0][:].indirect(l_n3[:]), ACT.Copy)
         nc.vector.tensor_copy(pair[0][:, W:], h2[0][:].indirect(l_n4[:]))
         larger[0] = sbuf("larger0", W, F32)
@@ -275,21 +277,20 @@ def tile_picked_mthhznhhaarcpor_none_p_kernel(
         nc.vector.tensor_tensor(smaller[0][:], pair[0][:, 0:W], pair[0][:, W:], ALU.min)
         put_larger(0)
         put_smaller(0)
-        empty(1)
         fetch(1)
-        empty(2)
-        subtract_pair(nc.gpsimd, 1)
+        empty(2, "pair0")
+        subtract_pair(1)
         rank_larger(1)
         put_larger(1)
-        rank_smaller(1)
-        put_smaller(1)
         fetch(2)
-        empty(3)
-        subtract_pair(nc.gpsimd, 2)
+        empty(3, "gap1")
+        subtract_pair(2)
         rank_larger(2)
         put_larger(2)
+        rank_smaller(1, "gap2")
+        put_smaller(1)
         fetch(3)
-        subtract_pair(nc.gpsimd, 3)
+        subtract_pair(3)
         rank_larger(3)
         put_larger(3)
         rank_smaller(2, "gap3")

from contextlib import ExitStack

import concourse.mybir as mybir

F32 = mybir.dt.float32
BF16 = mybir.dt.bfloat16
I32 = mybir.dt.int32
U32 = mybir.dt.uint32
U16 = mybir.dt.uint16
U8 = mybir.dt.uint8
FP8X4 = mybir.dt.float8_e4m3fn_x4
FP4X4 = mybir.dt.float4_e2m1fn_x4
ALU = mybir.AluOpType
ACT = mybir.ActivationFunctionType

P = 128
PACK = 4
T, G, S, W = 1024, 2048, 512, 256
HALF = S // 2
FLOPS = 5 * 2 * 512 * 512 * 512


def dealt_pair(dst, src, run):
    return (dst.rearrange("p (t c i) -> p c t i", t=PACK, i=run),
            src.rearrange("p (c i t) -> p c t i", t=PACK, i=run))


def tile_picked_mthhznhhaarcpor_none_p_kernel(
    tc, x_words, x_scales, d_words, d_scales, gn, w1_words, w1_scales, w2_words, w2_scales,
    offs, k1, hz, k2, hy, k3, n1, n2, hx, n3, n4, n5, n6, out,
):
    nc = tc.nc
    with ExitStack() as ctx:
        lists = ctx.enter_context(tc.tile_pool(name="lists", bufs=1))
        keep = ctx.enter_context(tc.tile_pool(name="keep", bufs=1))
        psum = ctx.enter_context(tc.psum_pool(name="psum", bufs=1))

        def sbuf(name, cols, dtype, tag=None):
            return keep.tile([P, cols], dtype, name=name, tag=tag or name, align_bytes=64)

        def load_list(name, src):
            tile = lists.tile(list(src.shape), U16, name=name)
            nc.sync.dma_start(tile[:], src)
            return tile

        def zeroed(name, cols, tag=None):
            tile = sbuf(name, cols, U8, tag)
            nc.vector.memset(tile[:].bitcast(I32), 0)
            return tile

        def move_rows(dst, dst_first, src, src_first=0):
            for s in range(4):
                nc.sync.dma_start(dst[dst_first + s : P : 32, :].bitcast(I32),
                                  src[src_first + 8 * s : P : 32, :].bitcast(I32))

        ds_table = sbuf("ds_table", G, U8)
        nc.gpsimd.memset(ds_table[:, : G // 2].bitcast(I32), 0)
        nc.vector.memset(ds_table[:, G // 2 :].bitcast(I32), 0)
        nc.sync.dma_start(ds_table[0:P:8, :].bitcast(I32), d_scales[0].bitcast(I32))
        d_lists = [load_list("k1", k1), load_list("k2", k2), load_list("k3", k3)]
        xs_table = zeroed("xs_table", T)
        nc.sync.dma_start(xs_table[0:P:8, :].bitcast(I32), x_scales[0].bitcast(I32))
        x_lists = [load_list("offs", offs), load_list("hz", hz), load_list("hy", hy)]
        xw_table = sbuf("xw_table", T, U32)
        nc.sync.dma_start(xw_table[:].bitcast(I32), x_words[0].rearrange("p n t -> p (n t)").bitcast(I32))
        dw_table = sbuf("dw_table", G, U32)
        nc.sync.dma_start(dw_table[:].bitcast(I32), d_words[0].rearrange("p n t -> p (n t)").bitcast(I32))
        ds_placed = zeroed("ds_placed", S, tag="slot_b")
        xs_placed = zeroed("xs_placed", 3 * S)
        hxs_placed = zeroed("hxs_placed", S)
        ws_raw = zeroed("ws_raw", S)
        ws_placed = [zeroed("w1s_placed", S), zeroed("w2s_placed", S)]

        for a in range(3):
            ds_picked = sbuf(f"ds_picked{a}", S, U8, tag="slot_a" if a == 2 else None)
            nc.vector.tensor_copy(ds_picked[:], ds_table[:].indirect(d_lists[a][:]))
            move_rows(ds_placed, 4 * a, ds_picked)
        xs_picked = sbuf("xs_picked", 3 * S, U8)
        for a in range(3):
            nc.vector.tensor_copy(xs_picked[:, a * S : (a + 1) * S], xs_table[:].indirect(x_lists[a][:]))
        move_rows(xs_placed, 0, xs_picked)

        gain_raw = sbuf("gain_raw", PACK, F32)
        nc.sync.dma_start(gain_raw[:], gn.rearrange("(p t) o -> p (t o)", t=PACK))
        l_n1, l_n2, l_hx = load_list("n1", n1), load_list("n2", n2), load_list("hx", hx)
        w_dealt = []
        for w, (words, scales) in enumerate(((w1_words, w1_scales), (w2_words, w2_scales))):
            raw = sbuf(f"w_raw{w}", 2 * S, U8)
            nc.sync.dma_start(raw[:].bitcast(I32), words[0].bitcast(I32))
            nc.sync.dma_start(ws_raw[w:P:8, :].bitcast(I32), scales[0].bitcast(I32))
            dealt = sbuf(f"w_dealt{w}", 2 * S, U8)
            nc.scalar.copy(*dealt_pair(dealt[:].bitcast(U16), raw[:].bitcast(U16), 8))
            w_dealt.append(dealt)
        l_n3, l_n4, l_n5, l_n6 = load_list("n3", n3), load_list("n4", n4), load_list("n5", n5), load_list("n6", n6)
        gain = sbuf("gain", PACK, F32)
        nc.scalar.activation(gain[:], gain_raw[:], ACT.Copy, scale=0.0625 * 0.75)

        ds_dealt = sbuf("ds_dealt", S, U8)
        h_banks = [psum.tile([P, S], F32, name=f"h_bank{t}", tag=f"bank{t}") for t in range(PACK)]
        dw_dealt, xw_picked = [], []

        def first_pass(a, t):
            cols = slice(t * P, (t + 1) * P)
            nc.tensor.matmul_mx(
                out=h_banks[t][:], lhsT=dw_dealt[a][:, cols].bitcast(FP8X4), lhsT_scale=ds_dealt[4 * a : P, cols],
                rhs=xw_picked[a][:].bitcast(FP8X4), rhs_scale=xs_placed[:, a * S : (a + 1) * S],
                start=(a == 0), stop=(a == 2))

        def pick_x(a, tag=None):
            xw_picked.append(sbuf(f"xw_picked{a}", S, U32, tag))
            nc.vector.tensor_copy(xw_picked[a][:], xw_table[:].indirect(x_lists[a][:]))

        def pick_d(a, tag):
            picked = sbuf(f"dw_picked{a}", S, U32, tag)
            nc.vector.tensor_copy(picked[:], dw_table[:].indirect(d_lists[a][:]))
            return picked

        def deal_d(a, picked):
            dw_dealt.append(sbuf(f"dw_dealt{a}", S, U32))
            nc.vector.tensor_copy(*dealt_pair(dw_dealt[a][:].bitcast(I32), picked[:].bitcast(I32), 4))

        pick_x(0)
        pick_x(1)
        nc.vector.tensor_copy(*dealt_pair(ds_dealt[:], ds_placed[:], 16))
        picked = [pick_d(0, "slot_a"), pick_d(1, "slot_b")]
        deal_d(0, picked[0])
        deal_d(1, picked[1])
        picked.append(pick_d(2, "slot_a"))
        pick_x(2, "slot_b")
        deal_d(2, picked[2])
        for t in (1, 3, 0, 2):
            for a in range(3):
                first_pass(a, t)

        hxw = sbuf("hxw", S, U32, tag="slot_a")
        nc.vector.tensor_copy(hxw[:], xw_table[:].indirect(l_hx[:]))

        h = [sbuf(f"h{t}", S, F32) for t in range(PACK)]
        terms = [sbuf(f"terms{t}", 4 * W, F32) for t in range(PACK)]
        z = [sbuf(f"z{t}", S * (2 - t % 2), F32) for t in range(PACK)]

        def empty_h(t):
            nc.scalar.activation(h[t][:], h_banks[t][:], ACT.Copy, scale=gain[:, t : t + 1])

        def fetch_n1(t):
            nc.scalar.activation(terms[t][:, 0:W], h[t][:].indirect(l_n1[:]), ACT.Copy)

        def fetch_pairs(t):
            fetch_n1(t)
            nc.scalar.activation(terms[t][:, W : 2 * W], h[t][:].indirect(l_n2[:]), ACT.Copy)

        def rescale(t):
            nc.scalar.activation(terms[t][:, 2 * W : 3 * W], terms[t][:, 0:W], ACT.Copy, scale=4.0 / 3.0)
            nc.scalar.activation(terms[t][:, 3 * W :], terms[t][:, W : 2 * W], ACT.Copy, scale=-4.0 / 3.0)

        def put_sum(t):
            nc.vector.tensor_tensor(z[t][:].indirect(l_n1[:]), terms[t][:, 0:W], terms[t][:, W : 2 * W], ALU.add)

        def put_diff(t):
            nc.vector.tensor_tensor(z[t][:].indirect(l_n2[:]), terms[t][:, 2 * W : 3 * W], terms[t][:, 3 * W :], ALU.add)

        z_bf = sbuf("z_bf", PACK * S, BF16)

        def round_pair(copy, t, c0, c1):
            dst = z_bf[:].rearrange("p (j u e) -> p j u e", u=2, e=2)[:, c0:c1, t // 2, :]
            src = z[t][:].rearrange("p (e j) -> p j e", e=2)[:, c0:c1, :]
            copy(dst, src)

        empty_h(1)
        fetch_n1(1)
        nc.vector.tensor_copy(terms[1][:, W : 2 * W], h[1][:].indirect(l_n2[:]))
        empty_h(3)
        put_sum(1)
        hxs_picked = sbuf("hxs_picked", S, U8, tag="h1")
        nc.vector.tensor_copy(hxs_picked[:], xs_table[:].indirect(l_hx[:]))
        move_rows(hxs_placed, 0, hxs_picked)
        rescale(1)
        put_diff(1)
        nc.sync.dma_start(z[0][:, S:], z[1][:])
        fetch_pairs(3)
        put_sum(3)
        ws_dealt = sbuf("ws_dealt", S, U8, tag="h3")
        nc.vector.tensor_copy(*dealt_pair(ws_dealt[:], ws_raw[:], 16))
        for w in range(2):
            move_rows(ws_placed[w], 0, ws_dealt, w)
        empty_h(0)
        rescale(3)
        put_diff(3)
        nc.sync.dma_start(z[2][:, S:], z[3][:])
        fetch_pairs(0)
        put_sum(0)
        empty_h(2)
        rescale(0)
        put_diff(0)
        fetch_pairs(2)
        put_sum(2)
        rescale(2)

        chunks = [[(0, HALF), (HALF, S)]] + [[(0, S)]] * 3
        h2_banks = []
        bank_no = 4
        for t in range(PACK):
            row = []
            for c0, c1 in chunks[t]:
                bank = psum.tile([P, c1 - c0], F32, name=f"h2_bank{t}_{c0}", tag=f"bank{bank_no % 8}")
                bank_no += 1
                nc.tensor.matmul_mx(
                    out=bank[:], lhsT=w_dealt[1][:, 2 * t * P : 2 * (t + 1) * P].bitcast(FP4X4),
                    lhsT_scale=ws_placed[1][:, t * P : (t + 1) * P],
                    rhs=hxw[:, c0:c1].bitcast(FP8X4), rhs_scale=hxs_placed[:, c0:c1], start=True, stop=False)
                row.append(bank)
            h2_banks.append(row)

        round_pair(nc.scalar.copy, 0, 0, S)
        put_diff(2)
        round_pair(nc.vector.tensor_copy, 2, 0, HALF)
        round_pair(nc.scalar.copy, 2, 384, S)
        round_pair(nc.vector.tensor_copy, 2, HALF, 384)
        zw = sbuf("zw", S, U32)
        zs = sbuf("zs", S, U8)
        for c0, c1 in chunks[0]:
            nc.vector.quantize_mx(out=zw[:, c0:c1].bitcast(FP8X4), scales=zs[:, c0:c1], in_=z_bf[:, PACK * c0 : PACK * c1])
        for t in range(PACK):
            for (c0, c1), bank in zip(chunks[t], h2_banks[t]):
                nc.tensor.matmul_mx(
                    out=bank[:], lhsT=w_dealt[0][:, 2 * t * P : 2 * (t + 1) * P].bitcast(FP4X4),
                    lhsT_scale=ws_placed[0][:, t * P : (t + 1) * P],
                    rhs=zw[:, c0:c1].bitcast(FP8X4), rhs_scale=zs[:, c0:c1], start=False, stop=True)

        h2 = [sbuf(f"h2_{t}", S, F32) for t in range(2)]
        pair = [sbuf(f"pair{t}", 2 * W, F32) for t in range(PACK)]
        ub2 = [sbuf(f"ub2_{t}", S, F32) for t in range(PACK)]
        out_rows = out.rearrange("(p t) j -> p t j", t=PACK)

        def empty(t, tag):
            h2.append(sbuf(f"h2_{t}", S, F32, tag))
            nc.scalar.copy(h2[t][:], h2_banks[t][0][:])

        def fetch(t):
            nc.scalar.activation(pair[t][:, 0:W], h2[t][:].indirect(l_n3[:]), ACT.Copy)
            nc.scalar.activation(pair[t][:, W:], h2[t][:].indirect(l_n4[:]), ACT.Copy)

        gap, rise, larger, smaller = {}, {}, {}, {}

        def subtract_pair(t):
            gap[t] = sbuf(f"gap{t}", W, F32)
            nc.gpsimd.tensor_tensor(gap[t][:], pair[t][:, W:], pair[t][:, 0:W], ALU.subtract)

        def rank_larger(t):
            rise[t] = sbuf(f"rise{t}", W, F32)
            larger[t] = sbuf(f"larger{t}", W, F32)
            nc.scalar.activation(rise[t][:], gap[t][:], ACT.Relu)
            nc.gpsimd.tensor_tensor(larger[t][:], pair[t][:, 0:W], rise[t][:], ALU.add)

        def rank_smaller(t, tag=None):
            smaller[t] = sbuf(f"smaller{t}", W, F32, tag)
            nc.gpsimd.tensor_tensor(smaller[t][:], pair[t][:, W:], rise[t][:], ALU.subtract)

        def put_larger(t):
            nc.vector.tensor_copy(ub2[t][:].indirect(l_n5[:]), larger[t][:])

        def put_smaller(t):
            nc.vector.tensor_copy(ub2[t][:].indirect(l_n6[:]), smaller[t][:])

        def finish(engine, t, res, c0, c1):
            engine.tensor_tensor(res[:, c0:c1], ub2[t][:, c0:c1], h2[t][:, c0:c1], ALU.subtract)
            nc.sync.dma_start(out_rows[:, t, c0:c1], res[:, c0:c1])

        nc.scalar.copy(h2[0][:, :HALF], h2_banks[0][0][:])
        nc.vector.tensor_copy(h2[0][:, HALF:], h2_banks[0][1][:])
        nc.vector.tensor_copy(h2[1][:], h2_banks[1][0][:])
        nc.scalar.activation(pair[0][:, 0:W], h2[0][:].indirect(l_n3[:]), ACT.Copy)
        nc.vector.tensor_copy(pair[0][:, W:], h2[0][:].indirect(l_n4[:]))
        larger[0] = sbuf("larger0", W, F32)
        smaller[0] = sbuf("smaller0", W, F32)
        nc.vector.tensor_tensor(larger[0][:], pair[0][:, 0:W], pair[0][:, W:], ALU.max)
        nc.vector.tensor_tensor(smaller[0][:], pair[0][:, 0:W], pair[0][:, W:], ALU.min)
        put_larger(0)
        put_smaller(0)
        fetch(1)
        empty(2, "pair0")
        subtract_pair(1)
        rank_larger(1)
        put_larger(1)
        fetch(2)
        empty(3, "gap1")
        subtract_pair(2)
        rank_larger(2)
        put_larger(2)
        rank_smaller(1, "gap2")
        put_smaller(1)
        fetch(3)
        subtract_pair(3)
        rank_larger(3)
        put_larger(3)
        rank_smaller(2, "gap3")
        put_smaller(2)
        rank_smaller(3)
        put_smaller(3)
        for t, tag in enumerate(("rise3", "pair3", None)):
            finish(nc.gpsimd, t, sbuf(f"res{t}", S, F32, tag), 0, S)
        last = sbuf("res3", S, F32)
        finish(nc.vector, PACK - 1, last, 0, HALF)
        finish(nc.vector, PACK - 1, last, HALF, S)
